import numpy as np
import ml_dtypes

BF16 = ml_dtypes.bfloat16


def bf(x):
    return np.asarray(x, np.float32).astype(BF16)


def f32(x):
    return np.asarray(x, np.float32)


def f64(x):
    return np.asarray(x).astype(np.float64)


def striped(idx):
    return np.tile(idx.reshape(-1, 16).T, (8, 1))


S, K, M, N, D, V = 4096, 256, 256, 2048, 2, 1024


def setup_inputs():
    return {"table": bf(np.random.standard_normal((K, S))), "w": bf(np.random.standard_normal((D, K, M)) / np.sqrt(D * K)), "b": f32(0.5 * np.random.standard_normal((M, 1))), "offs": striped(np.random.permutation(S)[:N])}


def reference(table, w, b, offs):
    idx = offs[:16].T.reshape(-1)
    x = f64(table)[:, idx]
    y = sum(f64(w)[t].T @ x[:, t * V : (t + 1) * V] for t in range(D))
    return np.tanh(y + f64(b))

@@ -1,0 +1,54 @@
+import concourse.mybir as mybir
+
+BF16, F32, U16 = mybir.dt.bfloat16, mybir.dt.float32, mybir.dt.uint16
+TANH = mybir.ActivationFunctionType.Tanh
+
+P = 128
+K, S = 256, 4096
+ENDS, M = 2, 256
+V = 1024
+PIECE = 512
+K_BLOCKS, M_BLOCKS, V_BLOCKS = K // P, M // P, V // PIECE
+
+FLOPS = 2 * K * M * ENDS * V
+
+
+def tile_gather_matmul_kernel(tc, table, w, b, offs, out):
+    nc = tc.nc
+    with (
+        tc.tile_pool(name="held", bufs=1) as held,
+        tc.tile_pool(name="results", bufs=2) as results,
+        tc.psum_pool(name="psum", bufs=2) as psum,
+    ):
+        offsets = held.tile([P, ENDS * V // 16], U16)
+        nc.sync.dma_start(offsets[:], offs)
+
+        weights = held.tile([P, ENDS, K_BLOCKS, M], BF16)
+        nc.scalar.dma_start(weights[:], w.rearrange("t (kb p) m -> p t kb m", p=P))
+
+        table_blocks = [held.tile([P, S], BF16, name=f"table{kb}") for kb in range(K_BLOCKS)]
+        nc.sync.dma_start(table_blocks[0][:], table[0:P, :])
+        nc.scalar.dma_start(table_blocks[1][:], table[P : 2 * P, :])
+
+        bias = held.tile([P, M_BLOCKS], F32)
+        nc.gpsimd.dma_start(bias[:], b.rearrange("(mb p) o -> p (mb o)", p=P))
+
+        for mb in range(M_BLOCKS):
+            for vb in range(V_BLOCKS):
+                bank = psum.tile([P, PIECE], F32)
+                terms = [(t, kb) for t in range(ENDS) for kb in range(K_BLOCKS)]
+                for t, kb in terms:
+                    first_column = (t * V + vb * PIECE) // 16
+                    piece = offsets[:, first_column : first_column + PIECE // 16]
+                    nc.tensor.matmul(
+                        bank[:],
+                        weights[:, t, kb, mb * P : (mb + 1) * P],
+                        table_blocks[kb][:].indirect(piece),
+                        start=(t, kb) == terms[0],
+                        stop=(t, kb) == terms[-1],
+                    )
+                result = results.tile([P, PIECE], F32)
+                nc.scalar.activation(result[:], bank[:], TANH, bias=bias[:, mb : mb + 1])
+                nc.sync.dma_start(
+                    out[mb * P : (mb + 1) * P, vb * PIECE : (vb + 1) * PIECE], result[:]
+                )

@@ -17,38 +17,46 @@ def tile_gather_matmul_kernel(tc, table, w, b, offs, out):
     nc = tc.nc
     with (
         tc.tile_pool(name="held", bufs=1) as held,
-        tc.tile_pool(name="results", bufs=2) as results,
-        tc.psum_pool(name="psum", bufs=2) as psum,
+        tc.psum_pool(name="psum", bufs=1) as psum,
     ):
         offsets = held.tile([P, ENDS * V // 16], U16)
         nc.sync.dma_start(offsets[:], offs)
 
+        table_blocks = [held.tile([P, S], BF16, name=f"table{kb}") for kb in range(K_BLOCKS)]
+        for kb in range(K_BLOCKS):
+            nc.sync.dma_start(table_blocks[kb][:], table[kb * P : (kb + 1) * P, :])
+
         weights = held.tile([P, ENDS, K_BLOCKS, M], BF16)
         nc.scalar.dma_start(weights[:], w.rearrange("t (kb p) m -> p t kb m", p=P))
 
-        table_blocks = [held.tile([P, S], BF16, name=f"table{kb}") for kb in range(K_BLOCKS)]
-        nc.sync.dma_start(table_blocks[0][:], table[0:P, :])
-        nc.scalar.dma_start(table_blocks[1][:], table[P : 2 * P, :])
-
         bias = held.tile([P, M_BLOCKS], F32)
-        nc.gpsimd.dma_start(bias[:], b.rearrange("(mb p) o -> p (mb o)", p=P))
+        nc.scalar.dma_start(bias[:], b.rearrange("(mb p) o -> p (mb o)", p=P))
 
-        for mb in range(M_BLOCKS):
-            for vb in range(V_BLOCKS):
-                bank = psum.tile([P, PIECE], F32)
-                terms = [(t, kb) for t in range(ENDS) for kb in range(K_BLOCKS)]
-                for t, kb in terms:
+        output_tiles = [(mb, vb) for mb in range(M_BLOCKS) for vb in range(V_BLOCKS)]
+        banks = {
+            (mb, vb): psum.tile([P, PIECE], F32, name=f"bank{mb}{vb}") for mb, vb in output_tiles
+        }
+        results = {
+            (mb, vb): held.tile([P, PIECE], F32, name=f"result{mb}{vb}") for mb, vb in output_tiles
+        }
+
+        for kb in range(K_BLOCKS):
+            for mb, vb in output_tiles:
+                for t in range(ENDS):
                     first_column = (t * V + vb * PIECE) // 16
                     piece = offsets[:, first_column : first_column + PIECE // 16]
                     nc.tensor.matmul(
-                        bank[:],
+                        banks[mb, vb][:],
                         weights[:, t, kb, mb * P : (mb + 1) * P],
                         table_blocks[kb][:].indirect(piece),
-                        start=(t, kb) == terms[0],
-                        stop=(t, kb) == terms[-1],
+                        start=(kb == 0 and t == 0),
+                        stop=(kb == K_BLOCKS - 1 and t == ENDS - 1),
                     )
-                result = results.tile([P, PIECE], F32)
-                nc.scalar.activation(result[:], bank[:], TANH, bias=bias[:, mb : mb + 1])
-                nc.sync.dma_start(
-                    out[mb * P : (mb + 1) * P, vb * PIECE : (vb + 1) * PIECE], result[:]
-                )
+                if kb == K_BLOCKS - 1:
+                    nc.scalar.activation(
+                        results[mb, vb][:], banks[mb, vb][:], TANH, bias=bias[:, mb : mb + 1]
+                    )
+                    nc.sync.dma_start(
+                        out[mb * P : (mb + 1) * P, vb * PIECE : (vb + 1) * PIECE],
+                        results[mb, vb][:],
+                    )

@@ -12,6 +12,8 @@ K_BLOCKS, M_BLOCKS, V_BLOCKS = K // P, M // P, V // PIECE
 
 FLOPS = 2 * K * M * ENDS * V
 
+WARM_UP_MATMULS = 8
+
 
 def tile_gather_matmul_kernel(tc, table, w, b, offs, out):
     nc = tc.nc
@@ -31,6 +33,12 @@ def tile_gather_matmul_kernel(tc, table, w, b, offs, out):
 
         bias = held.tile([P, M_BLOCKS], F32)
         nc.scalar.dma_start(bias[:], b.rearrange("(mb p) o -> p (mb o)", p=P))
+
+        zeros = held.tile([P, PIECE], BF16)
+        nc.vector.memset(zeros[:], 0.0)
+        unread = psum.tile([P, PIECE], F32)
+        for i in range(WARM_UP_MATMULS):
+            nc.tensor.matmul(unread[:], zeros[:, 0:P], zeros[:], start=True, stop=True)
 
         output_tiles = [(mb, vb) for mb in range(M_BLOCKS) for vb in range(V_BLOCKS)]
         banks = {

@@ -12,8 +12,6 @@ K_BLOCKS, M_BLOCKS, V_BLOCKS = K // P, M // P, V // PIECE
 
 FLOPS = 2 * K * M * ENDS * V
 
-WARM_UP_MATMULS = 8
-
 
 def tile_gather_matmul_kernel(tc, table, w, b, offs, out):
     nc = tc.nc
@@ -22,23 +20,16 @@ def tile_gather_matmul_kernel(tc, table, w, b, offs, out):
         tc.psum_pool(name="psum", bufs=1) as psum,
     ):
         offsets = held.tile([P, ENDS * V // 16], U16)
-        nc.sync.dma_start(offsets[:], offs)
-
         table_blocks = [held.tile([P, S], BF16, name=f"table{kb}") for kb in range(K_BLOCKS)]
-        for kb in range(K_BLOCKS):
-            nc.sync.dma_start(table_blocks[kb][:], table[kb * P : (kb + 1) * P, :])
-
-        weights = held.tile([P, ENDS, K_BLOCKS, M], BF16)
-        nc.scalar.dma_start(weights[:], w.rearrange("t (kb p) m -> p t kb m", p=P))
-
+        weights = [held.tile([P, ENDS, M], BF16, name=f"weights{kb}") for kb in range(K_BLOCKS)]
         bias = held.tile([P, M_BLOCKS], F32)
-        nc.scalar.dma_start(bias[:], b.rearrange("(mb p) o -> p (mb o)", p=P))
 
-        zeros = held.tile([P, PIECE], BF16)
-        nc.vector.memset(zeros[:], 0.0)
-        unread = psum.tile([P, PIECE], F32)
-        for i in range(WARM_UP_MATMULS):
-            nc.tensor.matmul(unread[:], zeros[:, 0:P], zeros[:], start=True, stop=True)
+        nc.sync.dma_start(offsets[:], offs)
+        nc.scalar.dma_start(weights[0][:], w[:, 0:P, :].rearrange("t p m -> p t m"))
+        nc.sync.dma_start(table_blocks[0][:], table[0:P, :])
+        nc.sync.dma_start(table_blocks[1][:], table[P : 2 * P, :])
+        nc.sync.dma_start(weights[1][:], w[:, P : 2 * P, :].rearrange("t p m -> p t m"))
+        nc.sync.dma_start(bias[:], b.rearrange("(mb p) o -> p (mb o)", p=P))
 
         output_tiles = [(mb, vb) for mb in range(M_BLOCKS) for vb in range(V_BLOCKS)]
         banks = {
@@ -55,7 +46,7 @@ def tile_gather_matmul_kernel(tc, table, w, b, offs, out):
                     piece = offsets[:, first_column : first_column + PIECE // 16]
                     nc.tensor.matmul(
                         banks[mb, vb][:],
-                        weights[:, t, kb, mb * P : (mb + 1) * P],
+                        weights[kb][:, t, mb * P : (mb + 1) * P],
                         table_blocks[kb][:].indirect(piece),
                         start=(kb == 0 and t == 0),
                         stop=(kb == K_BLOCKS - 1 and t == ENDS - 1),

@@ -9,6 +9,7 @@ ENDS, M = 2, 256
 V = 1024
 PIECE = 512
 K_BLOCKS, M_BLOCKS, V_BLOCKS = K // P, M // P, V // PIECE
+HALF = PIECE // 2
 
 FLOPS = 2 * K * M * ENDS * V
 
@@ -20,16 +21,17 @@ def tile_gather_matmul_kernel(tc, table, w, b, offs, out):
         tc.psum_pool(name="psum", bufs=1) as psum,
     ):
         offsets = held.tile([P, ENDS * V // 16], U16)
-        table_blocks = [held.tile([P, S], BF16, name=f"table{kb}") for kb in range(K_BLOCKS)]
-        weights = [held.tile([P, ENDS, M], BF16, name=f"weights{kb}") for kb in range(K_BLOCKS)]
-        bias = held.tile([P, M_BLOCKS], F32)
-
         nc.sync.dma_start(offsets[:], offs)
-        nc.scalar.dma_start(weights[0][:], w[:, 0:P, :].rearrange("t p m -> p t m"))
-        nc.sync.dma_start(table_blocks[0][:], table[0:P, :])
-        nc.sync.dma_start(table_blocks[1][:], table[P : 2 * P, :])
-        nc.sync.dma_start(weights[1][:], w[:, P : 2 * P, :].rearrange("t p m -> p t m"))
-        nc.sync.dma_start(bias[:], b.rearrange("(mb p) o -> p (mb o)", p=P))
+
+        table_blocks = [held.tile([P, S], BF16, name=f"table{kb}") for kb in range(K_BLOCKS)]
+        for kb in range(K_BLOCKS):
+            nc.sync.dma_start(table_blocks[kb][:], table[kb * P : (kb + 1) * P, :])
+
+        weights = held.tile([P, ENDS, K_BLOCKS, M], BF16)
+        nc.scalar.dma_start(weights[:], w.rearrange("t (kb p) m -> p t kb m", p=P))
+
+        bias = held.tile([P, M_BLOCKS], F32)
+        nc.scalar.dma_start(bias[:], b.rearrange("(mb p) o -> p (mb o)", p=P))
 
         output_tiles = [(mb, vb) for mb in range(M_BLOCKS) for vb in range(V_BLOCKS)]
         banks = {
@@ -46,16 +48,23 @@ def tile_gather_matmul_kernel(tc, table, w, b, offs, out):
                     piece = offsets[:, first_column : first_column + PIECE // 16]
                     nc.tensor.matmul(
                         banks[mb, vb][:],
-                        weights[kb][:, t, mb * P : (mb + 1) * P],
+                        weights[:, t, kb, mb * P : (mb + 1) * P],
                         table_blocks[kb][:].indirect(piece),
                         start=(kb == 0 and t == 0),
                         stop=(kb == K_BLOCKS - 1 and t == ENDS - 1),
                     )
                 if kb == K_BLOCKS - 1:
-                    nc.scalar.activation(
-                        results[mb, vb][:], banks[mb, vb][:], TANH, bias=bias[:, mb : mb + 1]
-                    )
-                    nc.sync.dma_start(
-                        out[mb * P : (mb + 1) * P, vb * PIECE : (vb + 1) * PIECE],
-                        results[mb, vb][:],
-                    )
+                    for first in (0, HALF):
+                        nc.scalar.activation(
+                            results[mb, vb][:, first : first + HALF],
+                            banks[mb, vb][:, first : first + HALF],
+                            TANH,
+                            bias=bias[:, mb : mb + 1],
+                        )
+                        nc.sync.dma_start(
+                            out[
+                                mb * P : (mb + 1) * P,
+                                vb * PIECE + first : vb * PIECE + first + HALF,
+                            ],
+                            results[mb, vb][:, first : first + HALF],
+                        )

@@ -41,30 +41,34 @@ def tile_gather_matmul_kernel(tc, table, w, b, offs, out):
             (mb, vb): held.tile([P, PIECE], F32, name=f"result{mb}{vb}") for mb, vb in output_tiles
         }
 
-        for kb in range(K_BLOCKS):
+        def product(kb, t, mb, vb):
+            first_column = (t * V + vb * PIECE) // 16
+            piece = offsets[:, first_column : first_column + PIECE // 16]
+            nc.tensor.matmul(
+                banks[mb, vb][:],
+                weights[:, t, kb, mb * P : (mb + 1) * P],
+                table_blocks[kb][:].indirect(piece),
+                start=(kb == 0 and t == 0),
+                stop=(kb == K_BLOCKS - 1 and t == ENDS - 1),
+            )
+
+        def finish(mb, vb):
+            for first in (0, HALF):
+                nc.scalar.activation(
+                    results[mb, vb][:, first : first + HALF],
+                    banks[mb, vb][:, first : first + HALF],
+                    TANH,
+                    bias=bias[:, mb : mb + 1],
+                )
+                nc.sync.dma_start(
+                    out[mb * P : (mb + 1) * P, vb * PIECE + first : vb * PIECE + first + HALF],
+                    results[mb, vb][:, first : first + HALF],
+                )
+
+        for t in range(ENDS):
             for mb, vb in output_tiles:
-                for t in range(ENDS):
-                    first_column = (t * V + vb * PIECE) // 16
-                    piece = offsets[:, first_column : first_column + PIECE // 16]
-                    nc.tensor.matmul(
-                        banks[mb, vb][:],
-                        weights[:, t, kb, mb * P : (mb + 1) * P],
-                        table_blocks[kb][:].indirect(piece),
-                        start=(kb == 0 and t == 0),
-                        stop=(kb == K_BLOCKS - 1 and t == ENDS - 1),
-                    )
-                if kb == K_BLOCKS - 1:
-                    for first in (0, HALF):
-                        nc.scalar.activation(
-                            results[mb, vb][:, first : first + HALF],
-                            banks[mb, vb][:, first : first + HALF],
-                            TANH,
-                            bias=bias[:, mb : mb + 1],
-                        )
-                        nc.sync.dma_start(
-                            out[
-                                mb * P : (mb + 1) * P,
-                                vb * PIECE + first : vb * PIECE + first + HALF,
-                            ],
-                            results[mb, vb][:, first : first + HALF],
-                        )
+                product(0, t, mb, vb)
+        for mb, vb in output_tiles:
+            for t in range(ENDS):
+                product(1, t, mb, vb)
+            finish(mb, vb)

@@ -24,11 +24,13 @@ def tile_gather_matmul_kernel(tc, table, w, b, offs, out):
         nc.sync.dma_start(offsets[:], offs)
 
         table_blocks = [held.tile([P, S], BF16, name=f"table{kb}") for kb in range(K_BLOCKS)]
-        for kb in range(K_BLOCKS):
-            nc.sync.dma_start(table_blocks[kb][:], table[kb * P : (kb + 1) * P, :])
+        weights = [held.tile([P, K_BLOCKS, M], BF16, name=f"weights{t}") for t in range(ENDS)]
 
-        weights = held.tile([P, ENDS, K_BLOCKS, M], BF16)
-        nc.scalar.dma_start(weights[:], w.rearrange("t (kb p) m -> p t kb m", p=P))
+        w_by_end = [w[t : t + 1].rearrange("t (kb p) m -> p (t kb) m", p=P) for t in range(ENDS)]
+        nc.scalar.dma_start(weights[0][:], w_by_end[0])
+        nc.sync.dma_start(table_blocks[0][:], table[0:P, :])
+        nc.sync.dma_start(weights[1][:], w_by_end[1])
+        nc.sync.dma_start(table_blocks[1][:], table[P : 2 * P, :])
 
         bias = held.tile([P, M_BLOCKS], F32)
         nc.scalar.dma_start(bias[:], b.rearrange("(mb p) o -> p (mb o)", p=P))
@@ -46,7 +48,7 @@ def tile_gather_matmul_kernel(tc, table, w, b, offs, out):
             piece = offsets[:, first_column : first_column + PIECE // 16]
             nc.tensor.matmul(
                 banks[mb, vb][:],
-                weights[:, t, kb, mb * P : (mb + 1) * P],
+                weights[t][:, kb, mb * P : (mb + 1) * P],
                 table_blocks[kb][:].indirect(piece),
                 start=(kb == 0 and t == 0),
                 stop=(kb == K_BLOCKS - 1 and t == ENDS - 1),

@@ -24,16 +24,26 @@ def tile_gather_matmul_kernel(tc, table, w, b, offs, out):
         nc.sync.dma_start(offsets[:], offs)
 
         table_blocks = [held.tile([P, S], BF16, name=f"table{kb}") for kb in range(K_BLOCKS)]
-        weights = [held.tile([P, K_BLOCKS, M], BF16, name=f"weights{t}") for t in range(ENDS)]
-
-        w_by_end = [w[t : t + 1].rearrange("t (kb p) m -> p (t kb) m", p=P) for t in range(ENDS)]
-        nc.scalar.dma_start(weights[0][:], w_by_end[0])
-        nc.sync.dma_start(table_blocks[0][:], table[0:P, :])
-        nc.sync.dma_start(weights[1][:], w_by_end[1])
-        nc.sync.dma_start(table_blocks[1][:], table[P : 2 * P, :])
-
+        weights = {
+            (t, kb): held.tile([P, M], BF16, name=f"weights{t}{kb}")
+            for t in range(ENDS)
+            for kb in range(K_BLOCKS)
+        }
         bias = held.tile([P, M_BLOCKS], F32)
-        nc.scalar.dma_start(bias[:], b.rearrange("(mb p) o -> p (mb o)", p=P))
+
+        w_rows = w.rearrange("t k m -> (t k) m")
+
+        def load_weights(queue, t, kb):
+            first_row = t * K + kb * P
+            queue.dma_start(weights[t, kb][:], w_rows[first_row : first_row + P, :])
+
+        load_weights(nc.scalar, 0, 0)
+        nc.sync.dma_start(table_blocks[0][:], table[0:P, :])
+        load_weights(nc.sync, 1, 0)
+        load_weights(nc.sync, 0, 1)
+        load_weights(nc.sync, 1, 1)
+        nc.sync.dma_start(table_blocks[1][:], table[P : 2 * P, :])
+        nc.sync.dma_start(bias[:], b.rearrange("(mb p) o -> p (mb o)", p=P))
 
         output_tiles = [(mb, vb) for mb in range(M_BLOCKS) for vb in range(V_BLOCKS)]
         banks = {
@@ -48,7 +58,7 @@ def tile_gather_matmul_kernel(tc, table, w, b, offs, out):
             piece = offsets[:, first_column : first_column + PIECE // 16]
             nc.tensor.matmul(
                 banks[mb, vb][:],
-                weights[t][:, kb, mb * P : (mb + 1) * P],
+                weights[t, kb][:, mb * P : (mb + 1) * P],
                 table_blocks[kb][:].indirect(piece),
                 start=(kb == 0 and t == 0),
                 stop=(kb == K_BLOCKS - 1 and t == ENDS - 1),

@@ -38,12 +38,12 @@ def tile_gather_matmul_kernel(tc, table, w, b, offs, out):
             queue.dma_start(weights[t, kb][:], w_rows[first_row : first_row + P, :])
 
         load_weights(nc.scalar, 0, 0)
+        nc.scalar.dma_start(bias[:], b.rearrange("(mb p) o -> p (mb o)", p=P))
         nc.sync.dma_start(table_blocks[0][:], table[0:P, :])
         load_weights(nc.sync, 1, 0)
         load_weights(nc.sync, 0, 1)
         load_weights(nc.sync, 1, 1)
         nc.sync.dma_start(table_blocks[1][:], table[P : 2 * P, :])
-        nc.sync.dma_start(bias[:], b.rearrange("(mb p) o -> p (mb o)", p=P))
 
         output_tiles = [(mb, vb) for mb in range(M_BLOCKS) for vb in range(V_BLOCKS)]
         banks = {

import concourse.mybir as mybir

BF16, F32, U16 = mybir.dt.bfloat16, mybir.dt.float32, mybir.dt.uint16
TANH = mybir.ActivationFunctionType.Tanh

P = 128
K, S = 256, 4096
ENDS, M = 2, 256
V = 1024
PIECE = 512
K_BLOCKS, M_BLOCKS, V_BLOCKS = K // P, M // P, V // PIECE
HALF = PIECE // 2

FLOPS = 2 * K * M * ENDS * V


def tile_gather_matmul_kernel(tc, table, w, b, offs, out):
    nc = tc.nc
    with (
        tc.tile_pool(name="held", bufs=1) as held,
        tc.psum_pool(name="psum", bufs=1) as psum,
    ):
        offsets = held.tile([P, ENDS * V // 16], U16)
        nc.sync.dma_start(offsets[:], offs)

        table_blocks = [held.tile([P, S], BF16, name=f"table{kb}") for kb in range(K_BLOCKS)]
        weights = {
            (t, kb): held.tile([P, M], BF16, name=f"weights{t}{kb}")
            for t in range(ENDS)
            for kb in range(K_BLOCKS)
        }
        bias = held.tile([P, M_BLOCKS], F32)

        w_rows = w.rearrange("t k m -> (t k) m")

        def load_weights(queue, t, kb):
            first_row = t * K + kb * P
            queue.dma_start(weights[t, kb][:], w_rows[first_row : first_row + P, :])

        load_weights(nc.scalar, 0, 0)
        nc.scalar.dma_start(bias[:], b.rearrange("(mb p) o -> p (mb o)", p=P))
        nc.sync.dma_start(table_blocks[0][:], table[0:P, :])
        load_weights(nc.sync, 1, 0)
        load_weights(nc.sync, 0, 1)
        load_weights(nc.sync, 1, 1)
        nc.sync.dma_start(table_blocks[1][:], table[P : 2 * P, :])

        output_tiles = [(mb, vb) for mb in range(M_BLOCKS) for vb in range(V_BLOCKS)]
        banks = {
            (mb, vb): psum.tile([P, PIECE], F32, name=f"bank{mb}{vb}") for mb, vb in output_tiles
        }
        results = {
            (mb, vb): held.tile([P, PIECE], F32, name=f"result{mb}{vb}") for mb, vb in output_tiles
        }

        def product(kb, t, mb, vb):
            first_column = (t * V + vb * PIECE) // 16
            piece = offsets[:, first_column : first_column + PIECE // 16]
            nc.tensor.matmul(
                banks[mb, vb][:],
                weights[t, kb][:, mb * P : (mb + 1) * P],
                table_blocks[kb][:].indirect(piece),
                start=(kb == 0 and t == 0),
                stop=(kb == K_BLOCKS - 1 and t == ENDS - 1),
            )

        def finish(mb, vb):
            for first in (0, HALF):
                nc.scalar.activation(
                    results[mb, vb][:, first : first + HALF],
                    banks[mb, vb][:, first : first + HALF],
                    TANH,
                    bias=bias[:, mb : mb + 1],
                )
                nc.sync.dma_start(
                    out[mb * P : (mb + 1) * P, vb * PIECE + first : vb * PIECE + first + HALF],
                    results[mb, vb][:, first : first + HALF],
                )

        for t in range(ENDS):
            for mb, vb in output_tiles:
                product(0, t, mb, vb)
        for mb, vb in output_tiles:
            for t in range(ENDS):
                product(1, t, mb, vb)
            finish(mb, vb)
